import numpy as np
import ml_dtypes


def mxq(x, axis, fmt="e4m3"):
    dtype, down = {"e4m3": (ml_dtypes.float8_e4m3fn, 7), "e5m2": (ml_dtypes.float8_e5m2, 14)}[fmt]
    v = np.moveaxis(np.asarray(x, np.float32).astype(ml_dtypes.bfloat16).astype(np.float64), axis, -1)
    blocks = v.reshape(v.shape[:-1] + (-1, 32))
    amax = np.abs(blocks).max(-1, keepdims=True)
    byte = np.maximum(np.where(amax > 0, np.frexp(amax)[1] - 1 + 127, 0) - down, 1)
    scale = np.exp2(byte - 127.0)
    codes = (blocks / scale).astype(np.float32).astype(dtype).astype(np.float64)
    return np.moveaxis((codes * scale).reshape(v.shape), -1, axis)


WIDE = False


def mx_kscale(k):
    if not WIDE:
        return np.ones(k)
    levels = np.array([10, -10, 5, -5, 0])
    if k % 512:
        return np.exp2(np.random.permutation(np.resize(levels, k // 32))).repeat(32)
    a = np.empty((k // 512, 16))
    for p in range(k // 512):
        a[p, :8] = np.random.permutation(np.resize(levels, 8))
        for g in range(8):
            far = levels[np.abs(levels - a[p, g]) >= 10]
            a[p, g + 8] = far[np.random.randint(len(far))]
    return np.exp2(a.ravel()).repeat(32)


def f64(x):
    return np.asarray(x).astype(np.float64)


def striped(idx):
    return np.tile(idx.reshape(-1, 16).T, (8, 1)).astype(np.uint16)


def unstriped(offs):
    return offs[:16].T.reshape(-1).astype(np.int64)


def striped8(idx):
    return np.concatenate([x.reshape(-1, 16).T for x in idx]).astype(np.uint16)


def runs(offs, k):
    lists = np.stack([offs[16 * r : 16 * r + 16].T.reshape(-1) for r in range(8)]).astype(np.int64)
    return lists[np.arange(k) % 512 // 64]


def pack_weight(w):
    k, n = w.shape
    w = f64(np.asarray(w, np.float32).astype(ml_dtypes.bfloat16)).reshape(k // 32, 32, n)
    amax = np.abs(w).max(1)
    byte = np.clip(np.where(amax > 0, np.frexp(amax)[1] - 1 + 127 - 7, 1), 1, 254)
    scaled = (w * np.exp2(127.0 - byte)[:, None, :]).reshape(k, n).astype(np.float32)
    words = np.ascontiguousarray(scaled.reshape(k // 512, 128, 4, n).transpose(0, 1, 3, 2)).astype(ml_dtypes.float8_e4m3fn).view(np.uint8)
    return words, np.ascontiguousarray(byte.astype(np.uint8).reshape(k // 512, 16, n))


def unpack_weight(words, scales):
    g, p, n, _ = words.shape
    vals = np.ascontiguousarray(words).view(ml_dtypes.float8_e4m3fn).astype(np.float64) * np.repeat(np.exp2(scales.astype(np.float64) - 127.0), 8, axis=1)[..., None]
    return vals.transpose(0, 1, 3, 2).reshape(g * 512, n)


K, T, S, N, G, H, U = 512, 2048, 256, 512, 2048, 512, 512


def setup_inputs():
    n = np.random.standard_normal
    s = mx_kscale(K)[:, None]
    u = mx_kscale(K)
    packed_xT = pack_weight(n((K, T)) * s)
    packed_dT = pack_weight(n((K, G)) / s)
    perm = np.random.permutation(U)
    return {
        "x_words": packed_xT[0],
        "x_scales": packed_xT[1],
        "d_words": packed_dT[0],
        "d_scales": packed_dT[1],
        "gn": (np.random.uniform(0.5, 1.5, (H, 1)) * u[:, None]).astype(np.float32),
        "w1": (n((H, N)) / np.sqrt(H) / u[:, None]).astype(np.float32),
        "offs": striped8(np.random.randint(0, T, (8, S))),
        "k1": striped8(np.random.randint(0, G, (8, H))),
        "n1": striped(perm[:S]),
        "n2": striped(perm[S:]),
        "n3": striped(np.random.permutation(S)),
    }


def reference(x_words, x_scales, d_words, d_scales, gn, w1, offs, k1, n1, n2, n3):
    d_k1 = unpack_weight(d_words, d_scales)[np.arange(K)[:, None], runs(k1, K)]
    xq = unpack_weight(x_words, x_scales)[np.arange(K)[:, None], runs(offs, K)]
    h = 0.0625 * (d_k1.T @ xq)
    z = f64(gn) * h
    h2 = mxq(f64(w1), 0, "e4m3").T @ mxq(z, 0, "e4m3")
    dn = np.minimum(h2, h2[:, unstriped(n3)])
    up = np.maximum(h2, h2[:, unstriped(n3)])
    ph = np.zeros((N, U))
    ph[:, unstriped(n1)] = up
    out = ph.copy()
    out[:, unstriped(n2)] = dn
    return out

@@ -1,0 +1,182 @@
+from contextlib import ExitStack
+
+import concourse.mybir as mybir
+
+K, T, S, N, G, H, U = 512, 2048, 256, 512, 2048, 512, 512
+FLOPS = 2 * K * H * S + 2 * H * N * S
+
+F32 = mybir.dt.float32
+BF16 = mybir.dt.bfloat16
+I32 = mybir.dt.int32
+U32 = mybir.dt.uint32
+U16 = mybir.dt.uint16
+U8 = mybir.dt.uint8
+FP8X4 = mybir.dt.float8_e4m3fn_x4
+ALU = mybir.AluOpType
+COPY = mybir.ActivationFunctionType.Copy
+
+P = 128
+PACK = 4
+HALF = S // 2
+SPARE = 16
+TILES = N // P
+
+
+def tile_picked_hpqipagmx_none_p_kernel(
+    tc, x_words, x_scales, d_words, d_scales, gn, w1, offs, k1, n1, n2, n3, out
+):
+    nc = tc.nc
+    with ExitStack() as ctx:
+        keep = ctx.enter_context(tc.tile_pool(name="keep", bufs=1))
+        psum = ctx.enter_context(tc.psum_pool(name="psum", bufs=1))
+
+        k1_t = keep.tile([P, H // 16], U16, name="k1_t")
+        offs_t = keep.tile([P, S // 16], U16, name="offs_t")
+        n1_t = keep.tile([P, S // 16], U16, name="n1_t")
+        n2_t = keep.tile([P, S // 16], U16, name="n2_t")
+        n3_t = keep.tile([P, S // 16], U16, name="n3_t")
+        d_tab = keep.tile([P, G], U32, name="d_tab", align_bytes=64)
+        x_tab = keep.tile([P, T], U32, name="x_tab", align_bytes=64)
+        d_stab = keep.tile([P, G], U8, name="d_stab", align_bytes=64)
+        x_stab = keep.tile([P, T], U8, name="x_stab", align_bytes=64)
+        gain = keep.tile([P, PACK], F32, name="gain")
+        w_raw = [keep.tile([P, PACK, N // 2], F32, name=f"w_raw{u}") for u in range(2)]
+
+        nc.vector.memset(d_stab[:].bitcast(I32), 0)
+        nc.vector.memset(x_stab[:].bitcast(I32), 0)
+
+        nc.sync.dma_start(k1_t[:], k1)
+        nc.scalar.dma_start(d_stab[0:P:8, :].bitcast(I32), d_scales[0].bitcast(I32))
+        nc.scalar.dma_start(x_stab[0:P:8, :].bitcast(I32), x_scales[0].bitcast(I32))
+        nc.sync.dma_start(d_tab[:].bitcast(I32), d_words[0].rearrange("p n t -> p (n t)").bitcast(I32))
+        nc.sync.dma_start(offs_t[:], offs)
+        nc.sync.dma_start(n3_t[:], n3)
+        nc.sync.dma_start(n1_t[:], n1)
+        nc.sync.dma_start(n2_t[:], n2)
+        nc.sync.dma_start(x_tab[:].bitcast(I32), x_words[0].rearrange("p n t -> p (n t)").bitcast(I32))
+        w_rows = w1.rearrange("(p j) n -> p j n", j=PACK)
+        for u in range(2):
+            nc.sync.dma_start(w_raw[u][:], w_rows[:, :, u * (N // 2) : (u + 1) * (N // 2)])
+        nc.gpsimd.dma_start(gain[:], gn.rearrange("(p t) o -> p (t o)", t=PACK))
+
+        pages = [keep.tile([P, U], F32, name=f"page{c}") for c in range(TILES)]
+        h2 = [keep.tile([P, S + SPARE], F32, name=f"h2_{c}") for c in range(TILES)]
+        for c in range(TILES):
+            nc.gpsimd.memset(h2[c][:, S:], 0.0)
+            nc.gpsimd.memset(pages[c][:], 0.0)
+
+        d_spick = keep.tile([P, H], U8, name="d_spick", align_bytes=64)
+        x_spick = keep.tile([P, S], U8, name="x_spick", align_bytes=64)
+        planes = keep.tile([P, H + S], U8, name="planes", align_bytes=64)
+        nc.vector.tensor_copy(d_spick[:], d_stab[:].indirect(k1_t[:]))
+        nc.vector.tensor_copy(x_spick[:], x_stab[:].indirect(offs_t[:]))
+        nc.vector.tensor_copy(
+            planes[:, :H].rearrange("p (t m) -> p m t", t=PACK),
+            d_spick[:].rearrange("p (m t) -> p m t", t=PACK),
+        )
+        nc.vector.tensor_copy(planes[:, H:].bitcast(I32), x_spick[:].bitcast(I32))
+        for s in range(1, 4):
+            nc.scalar.dma_start(planes[s:P:32, :].bitcast(I32), planes[8 * s : P : 32, :].bitcast(I32))
+
+        d_pick = keep.tile([P, H], U32, name="d_pick", align_bytes=64)
+        d_dealt = keep.tile([P, H], U32, name="d_dealt", align_bytes=64)
+        x_pick = keep.tile([P, S], U32, name="x_pick", align_bytes=64)
+        nc.vector.tensor_copy(d_pick[:], d_tab[:].indirect(k1_t[:]))
+        nc.vector.tensor_copy(
+            d_dealt[:].rearrange("p (t m) -> p m t", t=PACK),
+            d_pick[:].rearrange("p (m t) -> p m t", t=PACK),
+        )
+        nc.vector.tensor_copy(x_pick[:], x_tab[:].indirect(offs_t[:]))
+
+        w_codes = keep.tile([P, N], U32, name="w_codes", align_bytes=64)
+        w_scales = keep.tile([P, N], U8, name="w_scales", align_bytes=64)
+        w_first = keep.tile([P, N // 2, PACK], BF16, name="w_first", align_bytes=64)
+        for c in range(2):
+            cols = slice(c * P, (c + 1) * P)
+            nc.scalar.activation(w_first[:, cols, :], w_raw[0][:, :, cols].rearrange("p j n -> p n j"), COPY)
+            nc.vector.quantize_mx(
+                out=w_codes[:, cols].bitcast(FP8X4),
+                scales=w_scales[:, cols],
+                in_=w_first[:, cols, :].rearrange("p n j -> p (n j)"),
+            )
+
+        z = keep.tile([P, S, PACK], BF16, name="z", tag="grouped", align_bytes=64)
+        z_codes = keep.tile([P, S], U32, name="z_codes", align_bytes=64)
+        z_scales = keep.tile([P, S], U8, name="z_scales", align_bytes=64)
+        for u in range(2):
+            cols = slice(u * HALF, (u + 1) * HALF)
+            acc = psum.tile([P, PACK, HALF], F32, name=f"acc{u}")
+            for t in range(PACK):
+                nc.tensor.matmul_mx(
+                    out=acc[:, t, :],
+                    lhsT=d_dealt[:, t * P : (t + 1) * P].bitcast(FP8X4),
+                    lhsT_scale=planes[:, t * P : (t + 1) * P],
+                    rhs=x_pick[:, cols].bitcast(FP8X4),
+                    rhs_scale=planes[:, H + u * HALF : H + (u + 1) * HALF],
+                    start=True,
+                    stop=True,
+                )
+            nc.vector.scalar_tensor_tensor(
+                z[:, cols, :],
+                acc[:].rearrange("p t n -> p n t"),
+                0.0625,
+                gain[:].unsqueeze(1).to_broadcast([P, HALF, PACK]),
+                ALU.mult,
+                ALU.mult,
+            )
+        for u in range(2):
+            cols = slice(u * HALF, (u + 1) * HALF)
+            nc.vector.quantize_mx(
+                out=z_codes[:, cols].bitcast(FP8X4),
+                scales=z_scales[:, cols],
+                in_=z[:, cols, :].rearrange("p n t -> p (n t)"),
+            )
+
+        def product(c):
+            acc2 = psum.tile([P, S], F32, name=f"acc2_{c}")
+            nc.tensor.matmul_mx(
+                out=acc2[:],
+                lhsT=w_codes[:, c * P : (c + 1) * P].bitcast(FP8X4),
+                lhsT_scale=w_scales[:, c * P : (c + 1) * P],
+                rhs=z_codes[:].bitcast(FP8X4),
+                rhs_scale=z_scales[:],
+                start=True,
+                stop=True,
+            )
+            if c == 0:
+                nc.scalar.copy(h2[c][:, :S], acc2[:])
+            else:
+                nc.vector.tensor_copy(h2[c][:, :S], acc2[:])
+
+        def fetch(c):
+            other = keep.tile([P, S], F32, name=f"other{c}")
+            up = keep.tile([P, S], F32, name=f"up{c}")
+            dn = keep.tile([P, S], F32, name=f"dn{c}")
+            nc.scalar.activation(other[:], h2[c][:].indirect(n3_t[:]), COPY)
+            nc.vector.tensor_tensor(up[:], h2[c][:, :S], other[:], ALU.max)
+            nc.vector.tensor_tensor(dn[:], h2[c][:, :S], other[:], ALU.min)
+            return up, dn
+
+        def place(c, up, dn):
+            nc.scalar.activation(pages[c][:].indirect(n1_t[:]), up[:], COPY)
+            nc.scalar.activation(pages[c][:].indirect(n2_t[:]), dn[:], COPY)
+            nc.sync.dma_start(out[c * P : (c + 1) * P, :], pages[c][:])
+
+        product(0)
+        product(1)
+        pair = [fetch(0), fetch(1)]
+
+        w_second = keep.tile([P, N // 2, PACK], BF16, name="w_second", tag="grouped", align_bytes=64)
+        nc.vector.tensor_copy(w_second[:], w_raw[1][:].rearrange("p j n -> p n j"))
+        nc.vector.quantize_mx(
+            out=w_codes[:, N // 2 :].bitcast(FP8X4),
+            scales=w_scales[:, N // 2 :],
+            in_=w_second[:].rearrange("p n j -> p (n j)"),
+        )
+        product(2)
+        product(3)
+
+        for c in range(TILES):
+            place(c, *pair[c])
+            if c + 2 < TILES:
+                pair.append(fetch(c + 2))

@@ -40,67 +40,71 @@ def tile_picked_hpqipagmx_none_p_kernel(
         d_stab = keep.tile([P, G], U8, name="d_stab", align_bytes=64)
         x_stab = keep.tile([P, T], U8, name="x_stab", align_bytes=64)
         gain = keep.tile([P, PACK], F32, name="gain")
-        w_raw = [keep.tile([P, PACK, N // 2], F32, name=f"w_raw{u}") for u in range(2)]
+        w_raw0 = keep.tile([P, PACK, N // 2], F32, name="w_raw0")
+        planes = keep.tile([P, H + S], U8, name="planes", align_bytes=64)
 
-        nc.vector.memset(d_stab[:].bitcast(I32), 0)
+        nc.gpsimd.memset(d_stab[:].bitcast(I32), 0)
         nc.vector.memset(x_stab[:].bitcast(I32), 0)
 
         nc.sync.dma_start(k1_t[:], k1)
-        nc.scalar.dma_start(d_stab[0:P:8, :].bitcast(I32), d_scales[0].bitcast(I32))
-        nc.scalar.dma_start(x_stab[0:P:8, :].bitcast(I32), x_scales[0].bitcast(I32))
-        nc.sync.dma_start(d_tab[:].bitcast(I32), d_words[0].rearrange("p n t -> p (n t)").bitcast(I32))
+        nc.sync.dma_start(d_stab[0:P:8, :].bitcast(I32), d_scales[0].bitcast(I32))
         nc.sync.dma_start(offs_t[:], offs)
+        nc.sync.dma_start(x_stab[0:P:8, :].bitcast(I32), x_scales[0].bitcast(I32))
         nc.sync.dma_start(n3_t[:], n3)
         nc.sync.dma_start(n1_t[:], n1)
         nc.sync.dma_start(n2_t[:], n2)
+        nc.sync.dma_start(d_tab[:].bitcast(I32), d_words[0].rearrange("p n t -> p (n t)").bitcast(I32))
         nc.sync.dma_start(x_tab[:].bitcast(I32), x_words[0].rearrange("p n t -> p (n t)").bitcast(I32))
         w_rows = w1.rearrange("(p j) n -> p j n", j=PACK)
-        for u in range(2):
-            nc.sync.dma_start(w_raw[u][:], w_rows[:, :, u * (N // 2) : (u + 1) * (N // 2)])
-        nc.gpsimd.dma_start(gain[:], gn.rearrange("(p t) o -> p (t o)", t=PACK))
+        nc.sync.dma_start(w_raw0[:], w_rows[:, :, : N // 2])
 
         pages = [keep.tile([P, U], F32, name=f"page{c}") for c in range(TILES)]
         h2 = [keep.tile([P, S + SPARE], F32, name=f"h2_{c}") for c in range(TILES)]
+        nc.vector.memset(planes[:].bitcast(I32), 0)
+        nc.gpsimd.dma_start(gain[:], gn.rearrange("(p t) o -> p (t o)", t=PACK))
         for c in range(TILES):
-            nc.gpsimd.memset(h2[c][:, S:], 0.0)
-            nc.gpsimd.memset(pages[c][:], 0.0)
+            nc.vector.memset(h2[c][:, S:], 0.0)
 
         d_spick = keep.tile([P, H], U8, name="d_spick", align_bytes=64)
         x_spick = keep.tile([P, S], U8, name="x_spick", align_bytes=64)
-        planes = keep.tile([P, H + S], U8, name="planes", align_bytes=64)
+        apart = keep.tile([P, H + S], U8, name="apart", tag="staged", align_bytes=64)
         nc.vector.tensor_copy(d_spick[:], d_stab[:].indirect(k1_t[:]))
         nc.vector.tensor_copy(x_spick[:], x_stab[:].indirect(offs_t[:]))
         nc.vector.tensor_copy(
-            planes[:, :H].rearrange("p (t m) -> p m t", t=PACK),
-            d_spick[:].rearrange("p (m t) -> p m t", t=PACK),
+            apart[:, :H].rearrange("p (t b m) -> p b t m", t=PACK, m=16),
+            d_spick[:].rearrange("p (b m t) -> p b t m", t=PACK, m=16),
         )
-        nc.vector.tensor_copy(planes[:, H:].bitcast(I32), x_spick[:].bitcast(I32))
-        for s in range(1, 4):
-            nc.scalar.dma_start(planes[s:P:32, :].bitcast(I32), planes[8 * s : P : 32, :].bitcast(I32))
+        nc.vector.tensor_copy(apart[:, H:].bitcast(I32), x_spick[:].bitcast(I32))
+        for q in range(4):
+            nc.scalar.dma_start(
+                planes[32 * q : 32 * q + 4, :].bitcast(I32), apart[32 * q : 32 * q + 32 : 8, :].bitcast(I32)
+            )
+        w_raw1 = keep.tile([P, PACK, N // 2], F32, name="w_raw1", tag="staged", align_bytes=64)
+        nc.sync.dma_start(w_raw1[:], w_rows[:, :, N // 2 :])
 
         d_pick = keep.tile([P, H], U32, name="d_pick", align_bytes=64)
         d_dealt = keep.tile([P, H], U32, name="d_dealt", align_bytes=64)
         x_pick = keep.tile([P, S], U32, name="x_pick", align_bytes=64)
         nc.vector.tensor_copy(d_pick[:], d_tab[:].indirect(k1_t[:]))
         nc.vector.tensor_copy(
-            d_dealt[:].rearrange("p (t m) -> p m t", t=PACK),
-            d_pick[:].rearrange("p (m t) -> p m t", t=PACK),
+            d_dealt[:].rearrange("p (t b m) -> p b t m", t=PACK, m=4),
+            d_pick[:].rearrange("p (b m t) -> p b t m", t=PACK, m=4),
         )
         nc.vector.tensor_copy(x_pick[:], x_tab[:].indirect(offs_t[:]))
 
-        w_codes = keep.tile([P, N], U32, name="w_codes", align_bytes=64)
-        w_scales = keep.tile([P, N], U8, name="w_scales", align_bytes=64)
+        w_codes = keep.tile([P, N // 2], U32, name="w_codes", align_bytes=64)
+        w_scales = keep.tile([P, N // 2], U8, name="w_scales", align_bytes=64)
         w_first = keep.tile([P, N // 2, PACK], BF16, name="w_first", align_bytes=64)
         for c in range(2):
             cols = slice(c * P, (c + 1) * P)
-            nc.scalar.activation(w_first[:, cols, :], w_raw[0][:, :, cols].rearrange("p j n -> p n j"), COPY)
+            nc.scalar.activation(w_first[:, cols, :], w_raw0[:, :, cols].rearrange("p j n -> p n j"), COPY)
             nc.vector.quantize_mx(
                 out=w_codes[:, cols].bitcast(FP8X4),
                 scales=w_scales[:, cols],
                 in_=w_first[:, cols, :].rearrange("p n j -> p (n j)"),
             )
 
-        z = keep.tile([P, S, PACK], BF16, name="z", tag="grouped", align_bytes=64)
+        z = keep.tile([P, S, PACK], BF16, name="z", align_bytes=64)
         z_codes = keep.tile([P, S], U32, name="z_codes", align_bytes=64)
         z_scales = keep.tile([P, S], U8, name="z_scales", align_bytes=64)
         for u in range(2):
@@ -132,51 +136,76 @@ def tile_picked_hpqipagmx_none_p_kernel(
                 in_=z[:, cols, :].rearrange("p n t -> p (n t)"),
             )
 
-        def product(c):
-            acc2 = psum.tile([P, S], F32, name=f"acc2_{c}")
+        def product(c, codes, scales, cols):
+            acc2 = psum.tile([P, cols.stop - cols.start], F32, name=f"acc2_{c}_{cols.start}")
+            own = slice(c % 2 * P, (c % 2 + 1) * P)
             nc.tensor.matmul_mx(
                 out=acc2[:],
-                lhsT=w_codes[:, c * P : (c + 1) * P].bitcast(FP8X4),
-                lhsT_scale=w_scales[:, c * P : (c + 1) * P],
-                rhs=z_codes[:].bitcast(FP8X4),
-                rhs_scale=z_scales[:],
+                lhsT=codes[:, own].bitcast(FP8X4),
+                lhsT_scale=scales[:, own],
+                rhs=z_codes[:, cols].bitcast(FP8X4),
+                rhs_scale=z_scales[:, cols],
                 start=True,
                 stop=True,
             )
             if c == 0:
-                nc.scalar.copy(h2[c][:, :S], acc2[:])
+                nc.scalar.copy(h2[c][:, cols], acc2[:])
             else:
-                nc.vector.tensor_copy(h2[c][:, :S], acc2[:])
+                nc.vector.tensor_copy(h2[c][:, cols], acc2[:])
+
+        other, up, dn = {}, {}, {}
 
         def fetch(c):
-            other = keep.tile([P, S], F32, name=f"other{c}")
-            up = keep.tile([P, S], F32, name=f"up{c}")
-            dn = keep.tile([P, S], F32, name=f"dn{c}")
-            nc.scalar.activation(other[:], h2[c][:].indirect(n3_t[:]), COPY)
-            nc.vector.tensor_tensor(up[:], h2[c][:, :S], other[:], ALU.max)
-            nc.vector.tensor_tensor(dn[:], h2[c][:, :S], other[:], ALU.min)
-            return up, dn
+            other[c] = keep.tile([P, S], F32, name=f"other{c}", tag=f"other{c}", align_bytes=64)
+            nc.scalar.activation(other[c][:], h2[c][:].indirect(n3_t[:]), COPY)
 
-        def place(c, up, dn):
-            nc.scalar.activation(pages[c][:].indirect(n1_t[:]), up[:], COPY)
-            nc.scalar.activation(pages[c][:].indirect(n2_t[:]), dn[:], COPY)
+        def larger(c):
+            up[c] = keep.tile([P, S], F32, name=f"up{c}")
+            nc.vector.tensor_tensor(up[c][:], h2[c][:, :S], other[c][:], ALU.max)
+
+        def smaller(c):
+            dn[c] = keep.tile([P, S], F32, name=f"dn{c}", tag=f"dn{c}", align_bytes=64)
+            nc.vector.tensor_tensor(dn[c][:], h2[c][:, :S], other[c][:], ALU.min)
+
+        def place_up(c):
+            nc.scalar.activation(pages[c][:].indirect(n1_t[:]), up[c][:], COPY)
+
+        def place_dn(c):
+            nc.scalar.activation(pages[c][:].indirect(n2_t[:]), dn[c][:], COPY)
             nc.sync.dma_start(out[c * P : (c + 1) * P, :], pages[c][:])
 
-        product(0)
-        product(1)
-        pair = [fetch(0), fetch(1)]
+        product(0, w_codes, w_scales, slice(0, HALF))
+        product(0, w_codes, w_scales, slice(HALF, S))
+        product(1, w_codes, w_scales, slice(0, S))
+        fetch(0)
+        fetch(1)
+        larger(0)
+        larger(1)
+        smaller(0)
+        place_up(0)
+        place_up(1)
+        place_dn(0)
 
-        w_second = keep.tile([P, N // 2, PACK], BF16, name="w_second", tag="grouped", align_bytes=64)
-        nc.vector.tensor_copy(w_second[:], w_raw[1][:].rearrange("p j n -> p n j"))
+        w_second = keep.tile([P, N // 2, PACK], BF16, name="w_second", tag="other0", align_bytes=64)
+        v_codes = keep.tile([P, N // 2], U32, name="v_codes", tag="dn1", align_bytes=64)
+        v_scales = keep.tile([P, N // 2], U8, name="v_scales", align_bytes=64)
+        nc.vector.tensor_copy(w_second[:], w_raw1[:].rearrange("p j n -> p n j"))
         nc.vector.quantize_mx(
-            out=w_codes[:, N // 2 :].bitcast(FP8X4),
-            scales=w_scales[:, N // 2 :],
+            out=v_codes[:].bitcast(FP8X4),
+            scales=v_scales[:],
             in_=w_second[:].rearrange("p n j -> p (n j)"),
         )
-        product(2)
-        product(3)
-
-        for c in range(TILES):
-            place(c, *pair[c])
-            if c + 2 < TILES:
-                pair.append(fetch(c + 2))
+        product(2, v_codes, v_scales, slice(0, S))
+        product(3, v_codes, v_scales, slice(0, S))
+        fetch(2)
+        fetch(3)
+        smaller(1)
+        place_dn(1)
+        larger(2)
+        larger(3)
+        smaller(2)
+        smaller(3)
+        place_up(2)
+        place_up(3)
+        place_dn(2)
+        place_dn(3)

@@ -38,47 +38,42 @@ def tile_picked_hpqipagmx_none_p_kernel(
         d_tab = keep.tile([P, G], U32, name="d_tab", align_bytes=64)
         x_tab = keep.tile([P, T], U32, name="x_tab", align_bytes=64)
         d_stab = keep.tile([P, G], U8, name="d_stab", align_bytes=64)
-        x_stab = keep.tile([P, T], U8, name="x_stab", align_bytes=64)
-        gain = keep.tile([P, PACK], F32, name="gain")
-        w_raw0 = keep.tile([P, PACK, N // 2], F32, name="w_raw0")
+        x_stab = keep.tile([P, T], U8, name="x_stab", tag="x_stab", align_bytes=64)
+        gain = keep.tile([P, PACK], F32, name="gain", tag="gain", align_bytes=64)
         planes = keep.tile([P, H + S], U8, name="planes", align_bytes=64)
 
-        nc.gpsimd.memset(d_stab[:].bitcast(I32), 0)
+        nc.gpsimd.dma_start(gain[:], gn.rearrange("(p t) o -> p (t o)", t=PACK))
+        nc.vector.memset(d_stab[:].bitcast(I32), 0)
         nc.vector.memset(x_stab[:].bitcast(I32), 0)
 
+        d_rows = d_words[0].rearrange("p n t -> p (n t)").bitcast(I32)
         nc.sync.dma_start(k1_t[:], k1)
-        nc.sync.dma_start(d_stab[0:P:8, :].bitcast(I32), d_scales[0].bitcast(I32))
+        nc.sync.dma_start(d_tab[:, : G // 2].bitcast(I32), d_rows[:, : G // 2])
         nc.sync.dma_start(offs_t[:], offs)
+        nc.sync.dma_start(d_stab[0:P:8, :].bitcast(I32), d_scales[0].bitcast(I32))
         nc.sync.dma_start(x_stab[0:P:8, :].bitcast(I32), x_scales[0].bitcast(I32))
         nc.sync.dma_start(n3_t[:], n3)
+        nc.sync.dma_start(d_tab[:, G // 2 :].bitcast(I32), d_rows[:, G // 2 :])
+        nc.sync.dma_start(x_tab[:].bitcast(I32), x_words[0].rearrange("p n t -> p (n t)").bitcast(I32))
         nc.sync.dma_start(n1_t[:], n1)
         nc.sync.dma_start(n2_t[:], n2)
-        nc.sync.dma_start(d_tab[:].bitcast(I32), d_words[0].rearrange("p n t -> p (n t)").bitcast(I32))
-        nc.sync.dma_start(x_tab[:].bitcast(I32), x_words[0].rearrange("p n t -> p (n t)").bitcast(I32))
         w_rows = w1.rearrange("(p j) n -> p j n", j=PACK)
-        nc.sync.dma_start(w_raw0[:], w_rows[:, :, : N // 2])
 
         pages = [keep.tile([P, U], F32, name=f"page{c}") for c in range(TILES)]
         h2 = [keep.tile([P, S + SPARE], F32, name=f"h2_{c}") for c in range(TILES)]
         nc.vector.memset(planes[:].bitcast(I32), 0)
-        nc.gpsimd.dma_start(gain[:], gn.rearrange("(p t) o -> p (t o)", t=PACK))
         for c in range(TILES):
             nc.vector.memset(h2[c][:, S:], 0.0)
 
-        d_spick = keep.tile([P, H], U8, name="d_spick", align_bytes=64)
-        x_spick = keep.tile([P, S], U8, name="x_spick", align_bytes=64)
-        apart = keep.tile([P, H + S], U8, name="apart", tag="staged", align_bytes=64)
-        nc.vector.tensor_copy(d_spick[:], d_stab[:].indirect(k1_t[:]))
-        nc.vector.tensor_copy(x_spick[:], x_stab[:].indirect(offs_t[:]))
-        nc.vector.tensor_copy(
-            apart[:, :H].rearrange("p (t b m) -> p b t m", t=PACK, m=16),
-            d_spick[:].rearrange("p (b m t) -> p b t m", t=PACK, m=16),
-        )
-        nc.vector.tensor_copy(apart[:, H:].bitcast(I32), x_spick[:].bitcast(I32))
+        spick = keep.tile([P, H + S], U8, name="spick", tag="staged", align_bytes=64)
+        nc.vector.tensor_copy(spick[:, :H], d_stab[:].indirect(k1_t[:]))
+        nc.vector.tensor_copy(spick[:, H:], x_stab[:].indirect(offs_t[:]))
         for q in range(4):
             nc.scalar.dma_start(
-                planes[32 * q : 32 * q + 4, :].bitcast(I32), apart[32 * q : 32 * q + 32 : 8, :].bitcast(I32)
+                planes[32 * q : 32 * q + 4, :].bitcast(I32), spick[32 * q : 32 * q + 32 : 8, :].bitcast(I32)
             )
+        w_raw0 = keep.tile([P, PACK, N // 2], F32, name="w_raw0", tag="x_stab", align_bytes=64)
+        nc.scalar.dma_start(w_raw0[:], w_rows[:, :, : N // 2])
         w_raw1 = keep.tile([P, PACK, N // 2], F32, name="w_raw1", tag="staged", align_bytes=64)
         nc.sync.dma_start(w_raw1[:], w_rows[:, :, N // 2 :])
 
@@ -91,18 +86,25 @@ def tile_picked_hpqipagmx_none_p_kernel(
             d_pick[:].rearrange("p (b m t) -> p b t m", t=PACK, m=4),
         )
         nc.vector.tensor_copy(x_pick[:], x_tab[:].indirect(offs_t[:]))
+        d_plane = keep.tile([P, H], U8, name="d_plane", align_bytes=64)
+        for t in range(PACK):
+            nc.vector.tensor_copy(d_plane[:, t * P : (t + 1) * P], planes[:, t:H:PACK])
 
         w_codes = keep.tile([P, N // 2], U32, name="w_codes", align_bytes=64)
-        w_scales = keep.tile([P, N // 2], U8, name="w_scales", align_bytes=64)
+        w_scales = keep.tile([P, N // 2], U8, name="w_scales", tag="gain", align_bytes=64)
         w_first = keep.tile([P, N // 2, PACK], BF16, name="w_first", align_bytes=64)
         for c in range(2):
             cols = slice(c * P, (c + 1) * P)
             nc.scalar.activation(w_first[:, cols, :], w_raw0[:, :, cols].rearrange("p j n -> p n j"), COPY)
+
+        def quantise_first(c):
+            cols = slice(c * P, (c + 1) * P)
             nc.vector.quantize_mx(
                 out=w_codes[:, cols].bitcast(FP8X4),
                 scales=w_scales[:, cols],
                 in_=w_first[:, cols, :].rearrange("p n j -> p (n j)"),
             )
+
 
         z = keep.tile([P, S, PACK], BF16, name="z", align_bytes=64)
         z_codes = keep.tile([P, S], U32, name="z_codes", align_bytes=64)
@@ -114,7 +116,7 @@ def tile_picked_hpqipagmx_none_p_kernel(
                 nc.tensor.matmul_mx(
                     out=acc[:, t, :],
                     lhsT=d_dealt[:, t * P : (t + 1) * P].bitcast(FP8X4),
-                    lhsT_scale=planes[:, t * P : (t + 1) * P],
+                    lhsT_scale=d_plane[:, t * P : (t + 1) * P],
                     rhs=x_pick[:, cols].bitcast(FP8X4),
                     rhs_scale=planes[:, H + u * HALF : H + (u + 1) * HALF],
                     start=True,
@@ -135,6 +137,7 @@ def tile_picked_hpqipagmx_none_p_kernel(
                 scales=z_scales[:, cols],
                 in_=z[:, cols, :].rearrange("p n t -> p (n t)"),
             )
+            quantise_first(u)
 
         def product(c, codes, scales, cols):
             acc2 = psum.tile([P, cols.stop - cols.start], F32, name=f"acc2_{c}_{cols.start}")
@@ -148,7 +151,7 @@ def tile_picked_hpqipagmx_none_p_kernel(
                 start=True,
                 stop=True,
             )
-            if c == 0:
+            if c < 2:
                 nc.scalar.copy(h2[c][:, cols], acc2[:])
             else:
                 nc.vector.tensor_copy(h2[c][:, cols], acc2[:])
@@ -160,11 +163,11 @@ def tile_picked_hpqipagmx_none_p_kernel(
             nc.scalar.activation(other[c][:], h2[c][:].indirect(n3_t[:]), COPY)
 
         def larger(c):
-            up[c] = keep.tile([P, S], F32, name=f"up{c}")
+            up[c] = keep.tile([P, S], F32, name=f"up{c}", tag=f"value{c}", align_bytes=64)
             nc.vector.tensor_tensor(up[c][:], h2[c][:, :S], other[c][:], ALU.max)
 
-        def smaller(c):
-            dn[c] = keep.tile([P, S], F32, name=f"dn{c}", tag=f"dn{c}", align_bytes=64)
+        def smaller(c, tag):
+            dn[c] = keep.tile([P, S], F32, name=f"dn{c}", tag=tag, align_bytes=64)
             nc.vector.tensor_tensor(dn[c][:], h2[c][:, :S], other[c][:], ALU.min)
 
         def place_up(c):
@@ -181,31 +184,34 @@ def tile_picked_hpqipagmx_none_p_kernel(
         fetch(1)
         larger(0)
         larger(1)
-        smaller(0)
         place_up(0)
         place_up(1)
+        smaller(0, "value0")
         place_dn(0)
 
         w_second = keep.tile([P, N // 2, PACK], BF16, name="w_second", tag="other0", align_bytes=64)
-        v_codes = keep.tile([P, N // 2], U32, name="v_codes", tag="dn1", align_bytes=64)
+        v_codes = keep.tile([P, N // 2], U32, name="v_codes", tag="second", align_bytes=64)
         v_scales = keep.tile([P, N // 2], U8, name="v_scales", align_bytes=64)
-        nc.vector.tensor_copy(w_second[:], w_raw1[:].rearrange("p j n -> p n j"))
-        nc.vector.quantize_mx(
-            out=v_codes[:].bitcast(FP8X4),
-            scales=v_scales[:],
-            in_=w_second[:].rearrange("p n j -> p (n j)"),
-        )
-        product(2, v_codes, v_scales, slice(0, S))
-        product(3, v_codes, v_scales, slice(0, S))
+        for c in range(2):
+            cols = slice(c * P, (c + 1) * P)
+            nc.vector.tensor_copy(w_second[:, cols, :], w_raw1[:, :, cols].rearrange("p j n -> p n j"))
+        for c in range(2):
+            cols = slice(c * P, (c + 1) * P)
+            nc.vector.quantize_mx(
+                out=v_codes[:, cols].bitcast(FP8X4),
+                scales=v_scales[:, cols],
+                in_=w_second[:, cols, :].rearrange("p n j -> p (n j)"),
+            )
+            product(2 + c, v_codes, v_scales, slice(0, S))
         fetch(2)
         fetch(3)
-        smaller(1)
+        smaller(1, "second")
         place_dn(1)
         larger(2)
         larger(3)
-        smaller(2)
-        smaller(3)
         place_up(2)
         place_up(3)
+        smaller(2, "value2")
+        smaller(3, "value3")
         place_dn(2)
         place_dn(3)

@@ -42,18 +42,18 @@ def tile_picked_hpqipagmx_none_p_kernel(
         gain = keep.tile([P, PACK], F32, name="gain", tag="gain", align_bytes=64)
         planes = keep.tile([P, H + S], U8, name="planes", align_bytes=64)
 
-        nc.gpsimd.dma_start(gain[:], gn.rearrange("(p t) o -> p (t o)", t=PACK))
+        nc.scalar.dma_start(gain[:], gn.rearrange("(p t) o -> p (t o)", t=PACK))
         nc.vector.memset(d_stab[:].bitcast(I32), 0)
         nc.vector.memset(x_stab[:].bitcast(I32), 0)
 
         d_rows = d_words[0].rearrange("p n t -> p (n t)").bitcast(I32)
         nc.sync.dma_start(k1_t[:], k1)
-        nc.sync.dma_start(d_tab[:, : G // 2].bitcast(I32), d_rows[:, : G // 2])
+        nc.sync.dma_start(d_tab[:, : 3 * G // 8].bitcast(I32), d_rows[:, : 3 * G // 8])
         nc.sync.dma_start(offs_t[:], offs)
         nc.sync.dma_start(d_stab[0:P:8, :].bitcast(I32), d_scales[0].bitcast(I32))
         nc.sync.dma_start(x_stab[0:P:8, :].bitcast(I32), x_scales[0].bitcast(I32))
         nc.sync.dma_start(n3_t[:], n3)
-        nc.sync.dma_start(d_tab[:, G // 2 :].bitcast(I32), d_rows[:, G // 2 :])
+        nc.sync.dma_start(d_tab[:, 3 * G // 8 :].bitcast(I32), d_rows[:, 3 * G // 8 :])
         nc.sync.dma_start(x_tab[:].bitcast(I32), x_words[0].rearrange("p n t -> p (n t)").bitcast(I32))
         nc.sync.dma_start(n1_t[:], n1)
         nc.sync.dma_start(n2_t[:], n2)
@@ -69,7 +69,8 @@ def tile_picked_hpqipagmx_none_p_kernel(
         nc.vector.tensor_copy(spick[:, :H], d_stab[:].indirect(k1_t[:]))
         nc.vector.tensor_copy(spick[:, H:], x_stab[:].indirect(offs_t[:]))
         for q in range(4):
-            nc.scalar.dma_start(
+            queue = nc.scalar if q % 2 == 0 else nc.sync
+            queue.dma_start(
                 planes[32 * q : 32 * q + 4, :].bitcast(I32), spick[32 * q : 32 * q + 32 : 8, :].bitcast(I32)
             )
         w_raw0 = keep.tile([P, PACK, N // 2], F32, name="w_raw0", tag="x_stab", align_bytes=64)
@@ -151,20 +152,27 @@ def tile_picked_hpqipagmx_none_p_kernel(
                 start=True,
                 stop=True,
             )
-            if c < 2:
+            if c == 0:
                 nc.scalar.copy(h2[c][:, cols], acc2[:])
             else:
                 nc.vector.tensor_copy(h2[c][:, cols], acc2[:])
 
         other, up, dn = {}, {}, {}
 
-        def fetch(c):
+        def fetch(c, pieces=1):
             other[c] = keep.tile([P, S], F32, name=f"other{c}", tag=f"other{c}", align_bytes=64)
-            nc.scalar.activation(other[c][:], h2[c][:].indirect(n3_t[:]), COPY)
+            n = S // pieces
+            for lo in range(0, S, n):
+                nc.scalar.activation(
+                    other[c][:, lo : lo + n], h2[c][:].indirect(n3_t[:, lo // 16 : (lo + n) // 16]), COPY
+                )
 
-        def larger(c):
+        def larger(c, pieces=1):
             up[c] = keep.tile([P, S], F32, name=f"up{c}", tag=f"value{c}", align_bytes=64)
-            nc.vector.tensor_tensor(up[c][:], h2[c][:, :S], other[c][:], ALU.max)
+            n = S // pieces
+            for lo in range(0, S, n):
+                cols = slice(lo, lo + n)
+                nc.vector.tensor_tensor(up[c][:, cols], h2[c][:, cols], other[c][:, cols], ALU.max)
 
         def smaller(c, tag):
             dn[c] = keep.tile([P, S], F32, name=f"dn{c}", tag=tag, align_bytes=64)
@@ -180,9 +188,9 @@ def tile_picked_hpqipagmx_none_p_kernel(
         product(0, w_codes, w_scales, slice(0, HALF))
         product(0, w_codes, w_scales, slice(HALF, S))
         product(1, w_codes, w_scales, slice(0, S))
-        fetch(0)
+        fetch(0, 2)
         fetch(1)
-        larger(0)
+        larger(0, 2)
         larger(1)
         place_up(0)
         place_up(1)

@@ -48,12 +48,12 @@ def tile_picked_hpqipagmx_none_p_kernel(
 
         d_rows = d_words[0].rearrange("p n t -> p (n t)").bitcast(I32)
         nc.sync.dma_start(k1_t[:], k1)
-        nc.sync.dma_start(d_tab[:, : 3 * G // 8].bitcast(I32), d_rows[:, : 3 * G // 8])
+        nc.sync.dma_start(d_tab[:, : G // 4].bitcast(I32), d_rows[:, : G // 4])
         nc.sync.dma_start(offs_t[:], offs)
         nc.sync.dma_start(d_stab[0:P:8, :].bitcast(I32), d_scales[0].bitcast(I32))
         nc.sync.dma_start(x_stab[0:P:8, :].bitcast(I32), x_scales[0].bitcast(I32))
         nc.sync.dma_start(n3_t[:], n3)
-        nc.sync.dma_start(d_tab[:, 3 * G // 8 :].bitcast(I32), d_rows[:, 3 * G // 8 :])
+        nc.sync.dma_start(d_tab[:, G // 4 :].bitcast(I32), d_rows[:, G // 4 :])
         nc.sync.dma_start(x_tab[:].bitcast(I32), x_words[0].rearrange("p n t -> p (n t)").bitcast(I32))
         nc.sync.dma_start(n1_t[:], n1)
         nc.sync.dma_start(n2_t[:], n2)

from contextlib import ExitStack

import concourse.mybir as mybir

K, T, S, N, G, H, U = 512, 2048, 256, 512, 2048, 512, 512
FLOPS = 2 * K * H * S + 2 * H * N * S

F32 = mybir.dt.float32
BF16 = mybir.dt.bfloat16
I32 = mybir.dt.int32
U32 = mybir.dt.uint32
U16 = mybir.dt.uint16
U8 = mybir.dt.uint8
FP8X4 = mybir.dt.float8_e4m3fn_x4
ALU = mybir.AluOpType
COPY = mybir.ActivationFunctionType.Copy

P = 128
PACK = 4
HALF = S // 2
SPARE = 16
TILES = N // P


def tile_picked_hpqipagmx_none_p_kernel(
    tc, x_words, x_scales, d_words, d_scales, gn, w1, offs, k1, n1, n2, n3, out
):
    nc = tc.nc
    with ExitStack() as ctx:
        keep = ctx.enter_context(tc.tile_pool(name="keep", bufs=1))
        psum = ctx.enter_context(tc.psum_pool(name="psum", bufs=1))

        k1_t = keep.tile([P, H // 16], U16, name="k1_t")
        offs_t = keep.tile([P, S // 16], U16, name="offs_t")
        n1_t = keep.tile([P, S // 16], U16, name="n1_t")
        n2_t = keep.tile([P, S // 16], U16, name="n2_t")
        n3_t = keep.tile([P, S // 16], U16, name="n3_t")
        d_tab = keep.tile([P, G], U32, name="d_tab", align_bytes=64)
        x_tab = keep.tile([P, T], U32, name="x_tab", align_bytes=64)
        d_stab = keep.tile([P, G], U8, name="d_stab", align_bytes=64)
        x_stab = keep.tile([P, T], U8, name="x_stab", tag="x_stab", align_bytes=64)
        gain = keep.tile([P, PACK], F32, name="gain", tag="gain", align_bytes=64)
        planes = keep.tile([P, H + S], U8, name="planes", align_bytes=64)

        nc.scalar.dma_start(gain[:], gn.rearrange("(p t) o -> p (t o)", t=PACK))
        nc.vector.memset(d_stab[:].bitcast(I32), 0)
        nc.vector.memset(x_stab[:].bitcast(I32), 0)

        d_rows = d_words[0].rearrange("p n t -> p (n t)").bitcast(I32)
        nc.sync.dma_start(k1_t[:], k1)
        nc.sync.dma_start(d_tab[:, : G // 4].bitcast(I32), d_rows[:, : G // 4])
        nc.sync.dma_start(offs_t[:], offs)
        nc.sync.dma_start(d_stab[0:P:8, :].bitcast(I32), d_scales[0].bitcast(I32))
        nc.sync.dma_start(x_stab[0:P:8, :].bitcast(I32), x_scales[0].bitcast(I32))
        nc.sync.dma_start(n3_t[:], n3)
        nc.sync.dma_start(d_tab[:, G // 4 :].bitcast(I32), d_rows[:, G // 4 :])
        nc.sync.dma_start(x_tab[:].bitcast(I32), x_words[0].rearrange("p n t -> p (n t)").bitcast(I32))
        nc.sync.dma_start(n1_t[:], n1)
        nc.sync.dma_start(n2_t[:], n2)
        w_rows = w1.rearrange("(p j) n -> p j n", j=PACK)

        pages = [keep.tile([P, U], F32, name=f"page{c}") for c in range(TILES)]
        h2 = [keep.tile([P, S + SPARE], F32, name=f"h2_{c}") for c in range(TILES)]
        nc.vector.memset(planes[:].bitcast(I32), 0)
        for c in range(TILES):
            nc.vector.memset(h2[c][:, S:], 0.0)

        spick = keep.tile([P, H + S], U8, name="spick", tag="staged", align_bytes=64)
        nc.vector.tensor_copy(spick[:, :H], d_stab[:].indirect(k1_t[:]))
        nc.vector.tensor_copy(spick[:, H:], x_stab[:].indirect(offs_t[:]))
        for q in range(4):
            queue = nc.scalar if q % 2 == 0 else nc.sync
            queue.dma_start(
                planes[32 * q : 32 * q + 4, :].bitcast(I32), spick[32 * q : 32 * q + 32 : 8, :].bitcast(I32)
            )
        w_raw0 = keep.tile([P, PACK, N // 2], F32, name="w_raw0", tag="x_stab", align_bytes=64)
        nc.scalar.dma_start(w_raw0[:], w_rows[:, :, : N // 2])
        w_raw1 = keep.tile([P, PACK, N // 2], F32, name="w_raw1", tag="staged", align_bytes=64)
        nc.sync.dma_start(w_raw1[:], w_rows[:, :, N // 2 :])

        d_pick = keep.tile([P, H], U32, name="d_pick", align_bytes=64)
        d_dealt = keep.tile([P, H], U32, name="d_dealt", align_bytes=64)
        x_pick = keep.tile([P, S], U32, name="x_pick", align_bytes=64)
        nc.vector.tensor_copy(d_pick[:], d_tab[:].indirect(k1_t[:]))
        nc.vector.tensor_copy(
            d_dealt[:].rearrange("p (t b m) -> p b t m", t=PACK, m=4),
            d_pick[:].rearrange("p (b m t) -> p b t m", t=PACK, m=4),
        )
        nc.vector.tensor_copy(x_pick[:], x_tab[:].indirect(offs_t[:]))
        d_plane = keep.tile([P, H], U8, name="d_plane", align_bytes=64)
        for t in range(PACK):
            nc.vector.tensor_copy(d_plane[:, t * P : (t + 1) * P], planes[:, t:H:PACK])

        w_codes = keep.tile([P, N // 2], U32, name="w_codes", align_bytes=64)
        w_scales = keep.tile([P, N // 2], U8, name="w_scales", tag="gain", align_bytes=64)
        w_first = keep.tile([P, N // 2, PACK], BF16, name="w_first", align_bytes=64)
        for c in range(2):
            cols = slice(c * P, (c + 1) * P)
            nc.scalar.activation(w_first[:, cols, :], w_raw0[:, :, cols].rearrange("p j n -> p n j"), COPY)

        def quantise_first(c):
            cols = slice(c * P, (c + 1) * P)
            nc.vector.quantize_mx(
                out=w_codes[:, cols].bitcast(FP8X4),
                scales=w_scales[:, cols],
                in_=w_first[:, cols, :].rearrange("p n j -> p (n j)"),
            )


        z = keep.tile([P, S, PACK], BF16, name="z", align_bytes=64)
        z_codes = keep.tile([P, S], U32, name="z_codes", align_bytes=64)
        z_scales = keep.tile([P, S], U8, name="z_scales", align_bytes=64)
        for u in range(2):
            cols = slice(u * HALF, (u + 1) * HALF)
            acc = psum.tile([P, PACK, HALF], F32, name=f"acc{u}")
            for t in range(PACK):
                nc.tensor.matmul_mx(
                    out=acc[:, t, :],
                    lhsT=d_dealt[:, t * P : (t + 1) * P].bitcast(FP8X4),
                    lhsT_scale=d_plane[:, t * P : (t + 1) * P],
                    rhs=x_pick[:, cols].bitcast(FP8X4),
                    rhs_scale=planes[:, H + u * HALF : H + (u + 1) * HALF],
                    start=True,
                    stop=True,
                )
            nc.vector.scalar_tensor_tensor(
                z[:, cols, :],
                acc[:].rearrange("p t n -> p n t"),
                0.0625,
                gain[:].unsqueeze(1).to_broadcast([P, HALF, PACK]),
                ALU.mult,
                ALU.mult,
            )
        for u in range(2):
            cols = slice(u * HALF, (u + 1) * HALF)
            nc.vector.quantize_mx(
                out=z_codes[:, cols].bitcast(FP8X4),
                scales=z_scales[:, cols],
                in_=z[:, cols, :].rearrange("p n t -> p (n t)"),
            )
            quantise_first(u)

        def product(c, codes, scales, cols):
            acc2 = psum.tile([P, cols.stop - cols.start], F32, name=f"acc2_{c}_{cols.start}")
            own = slice(c % 2 * P, (c % 2 + 1) * P)
            nc.tensor.matmul_mx(
                out=acc2[:],
                lhsT=codes[:, own].bitcast(FP8X4),
                lhsT_scale=scales[:, own],
                rhs=z_codes[:, cols].bitcast(FP8X4),
                rhs_scale=z_scales[:, cols],
                start=True,
                stop=True,
            )
            if c == 0:
                nc.scalar.copy(h2[c][:, cols], acc2[:])
            else:
                nc.vector.tensor_copy(h2[c][:, cols], acc2[:])

        other, up, dn = {}, {}, {}

        def fetch(c, pieces=1):
            other[c] = keep.tile([P, S], F32, name=f"other{c}", tag=f"other{c}", align_bytes=64)
            n = S // pieces
            for lo in range(0, S, n):
                nc.scalar.activation(
                    other[c][:, lo : lo + n], h2[c][:].indirect(n3_t[:, lo // 16 : (lo + n) // 16]), COPY
                )

        def larger(c, pieces=1):
            up[c] = keep.tile([P, S], F32, name=f"up{c}", tag=f"value{c}", align_bytes=64)
            n = S // pieces
            for lo in range(0, S, n):
                cols = slice(lo, lo + n)
                nc.vector.tensor_tensor(up[c][:, cols], h2[c][:, cols], other[c][:, cols], ALU.max)

        def smaller(c, tag):
            dn[c] = keep.tile([P, S], F32, name=f"dn{c}", tag=tag, align_bytes=64)
            nc.vector.tensor_tensor(dn[c][:], h2[c][:, :S], other[c][:], ALU.min)

        def place_up(c):
            nc.scalar.activation(pages[c][:].indirect(n1_t[:]), up[c][:], COPY)

        def place_dn(c):
            nc.scalar.activation(pages[c][:].indirect(n2_t[:]), dn[c][:], COPY)
            nc.sync.dma_start(out[c * P : (c + 1) * P, :], pages[c][:])

        product(0, w_codes, w_scales, slice(0, HALF))
        product(0, w_codes, w_scales, slice(HALF, S))
        product(1, w_codes, w_scales, slice(0, S))
        fetch(0, 2)
        fetch(1)
        larger(0, 2)
        larger(1)
        place_up(0)
        place_up(1)
        smaller(0, "value0")
        place_dn(0)

        w_second = keep.tile([P, N // 2, PACK], BF16, name="w_second", tag="other0", align_bytes=64)
        v_codes = keep.tile([P, N // 2], U32, name="v_codes", tag="second", align_bytes=64)
        v_scales = keep.tile([P, N // 2], U8, name="v_scales", align_bytes=64)
        for c in range(2):
            cols = slice(c * P, (c + 1) * P)
            nc.vector.tensor_copy(w_second[:, cols, :], w_raw1[:, :, cols].rearrange("p j n -> p n j"))
        for c in range(2):
            cols = slice(c * P, (c + 1) * P)
            nc.vector.quantize_mx(
                out=v_codes[:, cols].bitcast(FP8X4),
                scales=v_scales[:, cols],
                in_=w_second[:, cols, :].rearrange("p n j -> p (n j)"),
            )
            product(2 + c, v_codes, v_scales, slice(0, S))
        fetch(2)
        fetch(3)
        smaller(1, "second")
        place_dn(1)
        larger(2)
        larger(3)
        place_up(2)
        place_up(3)
        smaller(2, "value2")
        smaller(3, "value3")
        place_dn(2)
        place_dn(3)
